import numpy as np
CORES = [48,49,50,51,52,53,54,55,72,73,74,75,76,77,78,79]
N = 16
COUNTS = [[0,32,0,4,0,0,0,4,0,8,8,8,4,8,0,0],[0,0,4,8,4,8,8,8,8,8,8,8,8,8,0,4],[8,32,0,0,4,4,0,4,0,0,0,4,4,8,0,0],[0,32,4,0,4,8,8,4,0,4,8,8,0,8,8,0],[8,32,0,8,0,8,4,4,4,4,0,4,0,8,4,4],[0,32,0,0,8,0,4,8,8,0,8,8,8,0,0,4],[4,32,4,4,8,0,0,0,4,8,4,0,0,8,0,0],[8,32,8,4,8,0,0,0,0,0,4,4,0,0,8,4],[4,32,0,8,4,0,4,8,0,4,0,4,4,8,0,4],[4,32,4,4,0,0,0,0,4,0,8,4,8,8,8,8],[8,32,4,4,8,0,0,8,4,4,0,0,0,4,8,4],[4,32,0,0,8,0,0,8,0,8,0,0,0,4,4,0],[0,32,0,4,0,8,8,4,8,0,4,8,0,8,0,4],[0,32,4,4,8,4,4,0,4,0,0,4,0,0,4,4],[0,32,0,8,0,4,4,8,8,8,8,8,8,8,0,0],[0,32,8,0,0,0,8,8,0,0,8,0,4,0,0,0]]
XW, YW = 104, 480
def setup_inputs(rng):
    return {"x": rng.standard_normal((N, 128, XW), dtype=np.float32)}
def reference(x):
    y = np.full((N, 128, YW), np.nan, x.dtype)
    fill = [0] * N
    for s in range(N):
        o = 0
        for d in range(N):
            c = COUNTS[s][d]
            y[d][:, fill[d]:fill[d] + c] = x[s][:, o:o + c]
            o += c; fill[d] += c
    return {"y": y}

@@ -1,0 +1,261 @@
+from concourse.bass import DstId, RemoteDMATransfer
+
+XW, YW, MW = 104, 480, 128
+SCRATCH = {
+    "xs": ("sbuf", [128, XW], "float32"),
+    "land": ("sbuf", [128, YW], "float32"),
+    "mrg": ("sbuf", [128, MW], "float32"),
+}
+SEMAPHORES = ["ld", "sent", "mj0", "mj1", "arr_on", "arr_x", "st_on", "st_x"]
+
+GATE_BIAS = 32.0
+PLANS = {}
+
+
+def popcount(m):
+    return bin(m).count("1")
+
+
+def row_weight(w):
+    return 1.0 + 4.0 * w / 512.0
+
+
+def allocate(calls, load, bias):
+    flat = []
+    for ci, call in enumerate(calls):
+        order = sorted(call, key=lambda t: not t["low"])
+        for k, t in enumerate(order):
+            flat.append((ci, t, sum(1 for u in order[k + 1:] if u["low"]), len(order) - k - 1))
+    best = {"key": None, "pick": None}
+
+    def rec(i, load, used, picks, fin):
+        if i == len(flat):
+            key = (max(v + b for v, b in zip(load, bias)), max(load), fin)
+            if best["key"] is None or key < best["key"]:
+                best["key"] = key
+                best["pick"] = list(picks)
+            return
+        ci, t, remlow, remall = flat[i]
+        if i > 0 and flat[i - 1][0] != ci:
+            used = 0
+        free = [e for e in range(8 if t["low"] else 16) if not (used >> e) & 1]
+        free.sort(key=lambda e: (load[e] + bias[e], -e))
+        for p in (16, 8, 4, 2, 1):
+            if p > len(free):
+                continue
+            m = 0
+            for e in free[:p]:
+                m |= 1 << e
+            u2 = used | m
+            if 8 - popcount(u2 & 0xFF) < remlow or 16 - popcount(u2) < remall:
+                continue
+            l2 = list(load)
+            for e in free[:p]:
+                l2[e] += 128 // p * row_weight(t["w"])
+            if best["key"] is not None and max(v + b for v, b in zip(l2, bias)) > best["key"][0] + 1e-9:
+                continue
+            picks.append(m)
+            rec(i + 1, l2, u2, picks, fin + max(l2[e] for e in free[:p]))
+            picks.pop()
+
+    rec(0, list(load), 0, [], 0.0)
+    out = list(load)
+    for (ci, t, a, b), m in zip(flat, best["pick"]):
+        t["mask"] = m
+        for e in range(16):
+            if (m >> e) & 1:
+                out[e] += 128 // popcount(m) * row_weight(t["w"])
+    return out
+
+
+def build_plan(cores, counts, topo, pick, only=None):
+    n = len(cores)
+    xo = [[sum(counts[s][:d]) for d in range(n)] for s in range(n)]
+    fill = [[sum(counts[t][d] for t in range(s)) for s in range(n + 1)] for d in range(n)]
+    chip_of = [topo.chip(c) for c in cores]
+    chips = sorted(set(chip_of))
+
+    def gates(ch):
+        return [c for c in range(8 * ch, 8 * ch + 8) if topo.may_write(c, 8 * (ch ^ 1))]
+
+    jobs = {}
+    paths = {}
+    xrows = {}
+    route = {}
+    for a in chips:
+        for b in chips:
+            if a == b:
+                continue
+            src = [r for r in range(n) if chip_of[r] == a]
+            dst = [r for r in range(n) if chip_of[r] == b]
+            own, hel = gates(a), gates(b ^ 1)
+            tot = {d: sum(counts[s][d] for s in src) for d in dst}
+            path = {}
+
+            def pkey(m):
+                return (topo.chip(m), topo.die(m))
+
+            def add_job(m, d, ss):
+                js = jobs.setdefault(m, [])
+                w = sum(counts[s][d] for s in ss)
+                j = {"merger": m, "d": d, "lo": ss[0], "w": w, "idx": len(js), "pos": sum(k["w"] for k in js)}
+                js.append(j)
+                path[pkey(m)] = path.get(pkey(m), 0) + w
+                for s in ss:
+                    route[(s, d)] = j
+
+            rest = []
+            for d in dst:
+                if 4 * tot[d] <= sum(tot.values()):
+                    rest.append(d)
+                    continue
+                run = []
+                for s in src + [None]:
+                    if s is not None and cores[s] not in own:
+                        run.append(s)
+                        continue
+                    if run:
+                        die = topo.die(cores[run[0]])
+                        m = min((h for h in hel if topo.die(h) == die), key=lambda h: len(jobs.get(h, [])))
+                        add_job(m, d, run)
+                        run = []
+                    if s is not None:
+                        route[(s, d)] = "direct"
+                        path[pkey(cores[s])] = path.get(pkey(cores[s]), 0) + counts[s][d]
+            for d in sorted(rest, key=lambda d: -tot[d]):
+                if tot[d] == 0:
+                    continue
+                pool = hel if d in pick[(a, b)] else own
+                m = min(pool, key=lambda m: (len(jobs.get(m, [])), path.get(pkey(m), 0)))
+                add_job(m, d, src)
+            paths[(a, b)] = max(path.values())
+
+    expect = {}
+
+    def bump(core, sem, v):
+        expect[(core, sem)] = expect.get((core, sem), 0) + v
+
+    sends, copies = {}, {}
+    for s in range(n):
+        if only is not None and chip_of[s] != only:
+            continue
+        cs = cores[s]
+        groups = {}
+        for d in range(n):
+            w = counts[s][d]
+            if w == 0 or d == s:
+                continue
+            t = {"w": w, "src": xo[s][d]}
+            if chip_of[d] == chip_of[s]:
+                t.update(dst=cores[d], buf="land", pos=fill[d][s], sem="arr_on", low=False, cls=1)
+            elif route[(s, d)] == "direct":
+                t.update(dst=cores[d], buf="land", pos=fill[d][s], sem="arr_x", low=True, cls=0)
+            else:
+                j = route[(s, d)]
+                t.update(dst=j["merger"], buf="mrg", pos=j["pos"] + fill[d][s] - fill[d][j["lo"]],
+                         sem="mj%d" % j["idx"], low=topo.chip(j["merger"]) != chip_of[s], cls=0)
+                if j["merger"] == cs:
+                    copies.setdefault(cs, []).append(t)
+                    bump(cs, t["sem"], 16)
+                    continue
+            groups.setdefault((t["cls"], -w), []).append(t)
+        load = [0.0] * 16
+        bias = [GATE_BIAS if e < 8 and cs in jobs else 0.0 for e in range(16)]
+        calls = []
+        for cls in (0, 1):
+            if cls == 1 and only is not None:
+                continue
+            part = [groups[k] for k in sorted(groups) if k[0] == cls]
+            if part:
+                load = allocate(part, load, bias if cls == 1 else [0.0] * 16)
+            if cls == 0:
+                xrows.setdefault(chip_of[s], []).append(max(load))
+            calls += part
+        sends[cs] = calls
+        for call in calls:
+            for t in call:
+                bump(t["dst"], t["sem"], popcount(t["mask"]))
+                bump(cs, "sent", popcount(t["mask"]))
+    for m, js in jobs.items():
+        for j in js:
+            bump(cores[j["d"]], "arr_x", 8)
+            bump(m, "sent", 8)
+    return {"paths": paths, "xrows": xrows, "fill": fill, "jobs": jobs, "sends": sends, "copies": copies,
+            "expect": expect, "chip_of": chip_of}
+
+
+def choose_plan(cores, counts, topo):
+    n = len(cores)
+    chips = sorted(set(topo.chip(c) for c in cores))
+    pick = {(a, b): frozenset() for a in chips for b in chips if a != b}
+    for a, b in sorted(pick):
+        dst = [r for r in range(n) if topo.chip(cores[r]) == b]
+        best = None
+        for bits in range(1 << len(dst)):
+            sub = frozenset(d for k, d in enumerate(dst) if (bits >> k) & 1)
+            trial = dict(pick)
+            trial[(a, b)] = sub
+            P = build_plan(cores, counts, topo, trial, a)
+            if any(len(js) > (1 if m in cores else 2) for m, js in P["jobs"].items() if topo.chip(m) in (a, b ^ 1)):
+                continue
+            xr = sorted(P["xrows"][a], reverse=True)
+            key = (xr[0], P["paths"][(a, b)], xr)
+            if best is None or key < best[0]:
+                best = (key, sub)
+        pick[(a, b)] = best[1]
+    return build_plan(cores, counts, topo, pick)
+
+
+def rank_program(g, core, T, topo):
+    counts = T.tables["COUNTS"]
+    cores = list(T.cores)
+    if "p" not in PLANS:
+        PLANS["p"] = choose_plan(cores, counts, topo)
+    P = PLANS["p"]
+    rank = T.rank_of(core)
+    jobs = P["jobs"].get(core, [])
+    if rank is None and not jobs:
+        return
+    expect = P["expect"]
+    n = len(cores)
+
+    def dst_id(c):
+        rid, pid, se = topo.addr(c)
+        return DstId(rid=rid, pnc=pid)
+
+    if rank is not None:
+        tot = sum(counts[rank])
+        g.sync.dma_start(T.xs[:, 0:tot], T.x[:, 0:tot]).then_inc(T.sem.ld, 16)
+        for t in P["copies"].get(core, []):
+            g.scalar.dma_start(T.mrg[:, t["pos"]:t["pos"] + t["w"]],
+                               T.x[:, t["src"]:t["src"] + t["w"]]).then_inc(T.sem[t["sem"]], 16)
+        g.wait_ge(T.sem.ld, 16)
+        for call in P["sends"][core]:
+            g.remote_dma_fused(
+                [RemoteDMATransfer(dst_ids=[dst_id(t["dst"])], dma_engine_mask=t["mask"], remote_sem=T.sem[t["sem"]],
+                                   src=T.xs[:, t["src"]:t["src"] + t["w"]],
+                                   dst=T[t["buf"]][:, t["pos"]:t["pos"] + t["w"]]) for t in call],
+                local_sem=T.sem.sent)
+
+    for j in jobs:
+        d = j["d"]
+        g.wait_ge(T.sem["mj%d" % j["idx"]], expect[(core, "mj%d" % j["idx"])])
+        rid, pid, se = topo.addr(cores[d])
+        at = P["fill"][d][j["lo"]]
+        g.remote_dma(T.land[:, at:at + j["w"]], T.mrg[:, j["pos"]:j["pos"] + j["w"]],
+                     T.sem.arr_x, T.sem.sent, pid, rid, 0xFF)
+
+    if rank is not None:
+        fill = P["fill"][rank]
+        mine = [s for s in range(n) if P["chip_of"][s] == P["chip_of"][rank]]
+        lo, hi = fill[mine[0]], fill[mine[-1] + 1]
+        other = (0, lo) if lo > 0 else (hi, fill[n])
+        if hi > lo:
+            g.sync.wait_ge(T.sem.arr_on, expect[(core, "arr_on")])
+            g.sync.dma_start(T.y[:, lo:hi], T.land[:, lo:hi]).then_inc(T.sem.st_on, 16)
+            g.sync.wait_ge(T.sem.st_on, 16)
+        if other[1] > other[0]:
+            g.scalar.wait_ge(T.sem.arr_x, expect[(core, "arr_x")])
+            g.scalar.dma_start(T.y[:, other[0]:other[1]], T.land[:, other[0]:other[1]]).then_inc(T.sem.st_x, 16)
+            g.scalar.wait_ge(T.sem.st_x, 16)
+    g.wait_ge(T.sem.sent, expect[(core, "sent")])

@@ -9,6 +9,7 @@ SCRATCH = {
 SEMAPHORES = ["ld", "sent", "mj0", "mj1", "arr_on", "arr_x", "st_on", "st_x"]
 
 GATE_BIAS = 32.0
+CHUNK = 2
 PLANS = {}
 
 
@@ -18,6 +19,18 @@ def popcount(m):
 
 def row_weight(w):
     return 1.0 + 4.0 * w / 512.0
+
+
+def chunks(call):
+    lows = [t for t in call if t["low"]]
+    highs = [t for t in call if not t["low"]]
+    order = []
+    while lows or highs:
+        if lows:
+            order.append(lows.pop(0))
+        if highs:
+            order.append(highs.pop(0))
+    return [order[i:i + CHUNK] for i in range(0, len(order), CHUNK)]
 
 
 def allocate(calls, load, bias):
@@ -165,7 +178,7 @@ def build_plan(cores, counts, topo, pick, only=None):
         for cls in (0, 1):
             if cls == 1 and only is not None:
                 continue
-            part = [groups[k] for k in sorted(groups) if k[0] == cls]
+            part = [c for k in sorted(groups) if k[0] == cls for c in chunks(groups[k])]
             if part:
                 load = allocate(part, load, bias if cls == 1 else [0.0] * 16)
             if cls == 0:

from concourse.bass import DstId, RemoteDMATransfer

XW, YW, MW = 104, 480, 128
SCRATCH = {
    "xs": ("sbuf", [128, XW], "float32"),
    "land": ("sbuf", [128, YW], "float32"),
    "mrg": ("sbuf", [128, MW], "float32"),
}
SEMAPHORES = ["ld", "sent", "mj0", "mj1", "arr_on", "arr_x", "st_on", "st_x"]

GATE_BIAS = 32.0
CHUNK = 2
PLANS = {}


def popcount(m):
    return bin(m).count("1")


def row_weight(w):
    return 1.0 + 4.0 * w / 512.0


def chunks(call):
    lows = [t for t in call if t["low"]]
    highs = [t for t in call if not t["low"]]
    order = []
    while lows or highs:
        if lows:
            order.append(lows.pop(0))
        if highs:
            order.append(highs.pop(0))
    return [order[i:i + CHUNK] for i in range(0, len(order), CHUNK)]


def allocate(calls, load, bias):
    flat = []
    for ci, call in enumerate(calls):
        order = sorted(call, key=lambda t: not t["low"])
        for k, t in enumerate(order):
            flat.append((ci, t, sum(1 for u in order[k + 1:] if u["low"]), len(order) - k - 1))
    best = {"key": None, "pick": None}

    def rec(i, load, used, picks, fin):
        if i == len(flat):
            key = (max(v + b for v, b in zip(load, bias)), max(load), fin)
            if best["key"] is None or key < best["key"]:
                best["key"] = key
                best["pick"] = list(picks)
            return
        ci, t, remlow, remall = flat[i]
        if i > 0 and flat[i - 1][0] != ci:
            used = 0
        free = [e for e in range(8 if t["low"] else 16) if not (used >> e) & 1]
        free.sort(key=lambda e: (load[e] + bias[e], -e))
        for p in (16, 8, 4, 2, 1):
            if p > len(free):
                continue
            m = 0
            for e in free[:p]:
                m |= 1 << e
            u2 = used | m
            if 8 - popcount(u2 & 0xFF) < remlow or 16 - popcount(u2) < remall:
                continue
            l2 = list(load)
            for e in free[:p]:
                l2[e] += 128 // p * row_weight(t["w"])
            if best["key"] is not None and max(v + b for v, b in zip(l2, bias)) > best["key"][0] + 1e-9:
                continue
            picks.append(m)
            rec(i + 1, l2, u2, picks, fin + max(l2[e] for e in free[:p]))
            picks.pop()

    rec(0, list(load), 0, [], 0.0)
    out = list(load)
    for (ci, t, a, b), m in zip(flat, best["pick"]):
        t["mask"] = m
        for e in range(16):
            if (m >> e) & 1:
                out[e] += 128 // popcount(m) * row_weight(t["w"])
    return out


def build_plan(cores, counts, topo, pick, only=None):
    n = len(cores)
    xo = [[sum(counts[s][:d]) for d in range(n)] for s in range(n)]
    fill = [[sum(counts[t][d] for t in range(s)) for s in range(n + 1)] for d in range(n)]
    chip_of = [topo.chip(c) for c in cores]
    chips = sorted(set(chip_of))

    def gates(ch):
        return [c for c in range(8 * ch, 8 * ch + 8) if topo.may_write(c, 8 * (ch ^ 1))]

    jobs = {}
    paths = {}
    xrows = {}
    route = {}
    for a in chips:
        for b in chips:
            if a == b:
                continue
            src = [r for r in range(n) if chip_of[r] == a]
            dst = [r for r in range(n) if chip_of[r] == b]
            own, hel = gates(a), gates(b ^ 1)
            tot = {d: sum(counts[s][d] for s in src) for d in dst}
            path = {}

            def pkey(m):
                return (topo.chip(m), topo.die(m))

            def add_job(m, d, ss):
                js = jobs.setdefault(m, [])
                w = sum(counts[s][d] for s in ss)
                j = {"merger": m, "d": d, "lo": ss[0], "w": w, "idx": len(js), "pos": sum(k["w"] for k in js)}
                js.append(j)
                path[pkey(m)] = path.get(pkey(m), 0) + w
                for s in ss:
                    route[(s, d)] = j

            rest = []
            for d in dst:
                if 4 * tot[d] <= sum(tot.values()):
                    rest.append(d)
                    continue
                run = []
                for s in src + [None]:
                    if s is not None and cores[s] not in own:
                        run.append(s)
                        continue
                    if run:
                        die = topo.die(cores[run[0]])
                        m = min((h for h in hel if topo.die(h) == die), key=lambda h: len(jobs.get(h, [])))
                        add_job(m, d, run)
                        run = []
                    if s is not None:
                        route[(s, d)] = "direct"
                        path[pkey(cores[s])] = path.get(pkey(cores[s]), 0) + counts[s][d]
            for d in sorted(rest, key=lambda d: -tot[d]):
                if tot[d] == 0:
                    continue
                pool = hel if d in pick[(a, b)] else own
                m = min(pool, key=lambda m: (len(jobs.get(m, [])), path.get(pkey(m), 0)))
                add_job(m, d, src)
            paths[(a, b)] = max(path.values())

    expect = {}

    def bump(core, sem, v):
        expect[(core, sem)] = expect.get((core, sem), 0) + v

    sends, copies = {}, {}
    for s in range(n):
        if only is not None and chip_of[s] != only:
            continue
        cs = cores[s]
        groups = {}
        for d in range(n):
            w = counts[s][d]
            if w == 0 or d == s:
                continue
            t = {"w": w, "src": xo[s][d]}
            if chip_of[d] == chip_of[s]:
                t.update(dst=cores[d], buf="land", pos=fill[d][s], sem="arr_on", low=False, cls=1)
            elif route[(s, d)] == "direct":
                t.update(dst=cores[d], buf="land", pos=fill[d][s], sem="arr_x", low=True, cls=0)
            else:
                j = route[(s, d)]
                t.update(dst=j["merger"], buf="mrg", pos=j["pos"] + fill[d][s] - fill[d][j["lo"]],
                         sem="mj%d" % j["idx"], low=topo.chip(j["merger"]) != chip_of[s], cls=0)
                if j["merger"] == cs:
                    copies.setdefault(cs, []).append(t)
                    bump(cs, t["sem"], 16)
                    continue
            groups.setdefault((t["cls"], -w), []).append(t)
        load = [0.0] * 16
        bias = [GATE_BIAS if e < 8 and cs in jobs else 0.0 for e in range(16)]
        calls = []
        for cls in (0, 1):
            if cls == 1 and only is not None:
                continue
            part = [c for k in sorted(groups) if k[0] == cls for c in chunks(groups[k])]
            if part:
                load = allocate(part, load, bias if cls == 1 else [0.0] * 16)
            if cls == 0:
                xrows.setdefault(chip_of[s], []).append(max(load))
            calls += part
        sends[cs] = calls
        for call in calls:
            for t in call:
                bump(t["dst"], t["sem"], popcount(t["mask"]))
                bump(cs, "sent", popcount(t["mask"]))
    for m, js in jobs.items():
        for j in js:
            bump(cores[j["d"]], "arr_x", 8)
            bump(m, "sent", 8)
    return {"paths": paths, "xrows": xrows, "fill": fill, "jobs": jobs, "sends": sends, "copies": copies,
            "expect": expect, "chip_of": chip_of}


def choose_plan(cores, counts, topo):
    n = len(cores)
    chips = sorted(set(topo.chip(c) for c in cores))
    pick = {(a, b): frozenset() for a in chips for b in chips if a != b}
    for a, b in sorted(pick):
        dst = [r for r in range(n) if topo.chip(cores[r]) == b]
        best = None
        for bits in range(1 << len(dst)):
            sub = frozenset(d for k, d in enumerate(dst) if (bits >> k) & 1)
            trial = dict(pick)
            trial[(a, b)] = sub
            P = build_plan(cores, counts, topo, trial, a)
            if any(len(js) > (1 if m in cores else 2) for m, js in P["jobs"].items() if topo.chip(m) in (a, b ^ 1)):
                continue
            xr = sorted(P["xrows"][a], reverse=True)
            key = (xr[0], P["paths"][(a, b)], xr)
            if best is None or key < best[0]:
                best = (key, sub)
        pick[(a, b)] = best[1]
    return build_plan(cores, counts, topo, pick)


def rank_program(g, core, T, topo):
    counts = T.tables["COUNTS"]
    cores = list(T.cores)
    if "p" not in PLANS:
        PLANS["p"] = choose_plan(cores, counts, topo)
    P = PLANS["p"]
    rank = T.rank_of(core)
    jobs = P["jobs"].get(core, [])
    if rank is None and not jobs:
        return
    expect = P["expect"]
    n = len(cores)

    def dst_id(c):
        rid, pid, se = topo.addr(c)
        return DstId(rid=rid, pnc=pid)

    if rank is not None:
        tot = sum(counts[rank])
        g.sync.dma_start(T.xs[:, 0:tot], T.x[:, 0:tot]).then_inc(T.sem.ld, 16)
        for t in P["copies"].get(core, []):
            g.scalar.dma_start(T.mrg[:, t["pos"]:t["pos"] + t["w"]],
                               T.x[:, t["src"]:t["src"] + t["w"]]).then_inc(T.sem[t["sem"]], 16)
        g.wait_ge(T.sem.ld, 16)
        for call in P["sends"][core]:
            g.remote_dma_fused(
                [RemoteDMATransfer(dst_ids=[dst_id(t["dst"])], dma_engine_mask=t["mask"], remote_sem=T.sem[t["sem"]],
                                   src=T.xs[:, t["src"]:t["src"] + t["w"]],
                                   dst=T[t["buf"]][:, t["pos"]:t["pos"] + t["w"]]) for t in call],
                local_sem=T.sem.sent)

    for j in jobs:
        d = j["d"]
        g.wait_ge(T.sem["mj%d" % j["idx"]], expect[(core, "mj%d" % j["idx"])])
        rid, pid, se = topo.addr(cores[d])
        at = P["fill"][d][j["lo"]]
        g.remote_dma(T.land[:, at:at + j["w"]], T.mrg[:, j["pos"]:j["pos"] + j["w"]],
                     T.sem.arr_x, T.sem.sent, pid, rid, 0xFF)

    if rank is not None:
        fill = P["fill"][rank]
        mine = [s for s in range(n) if P["chip_of"][s] == P["chip_of"][rank]]
        lo, hi = fill[mine[0]], fill[mine[-1] + 1]
        other = (0, lo) if lo > 0 else (hi, fill[n])
        if hi > lo:
            g.sync.wait_ge(T.sem.arr_on, expect[(core, "arr_on")])
            g.sync.dma_start(T.y[:, lo:hi], T.land[:, lo:hi]).then_inc(T.sem.st_on, 16)
            g.sync.wait_ge(T.sem.st_on, 16)
        if other[1] > other[0]:
            g.scalar.wait_ge(T.sem.arr_x, expect[(core, "arr_x")])
            g.scalar.dma_start(T.y[:, other[0]:other[1]], T.land[:, other[0]:other[1]]).then_inc(T.sem.st_x, 16)
            g.scalar.wait_ge(T.sem.st_x, 16)
    g.wait_ge(T.sem.sent, expect[(core, "sent")])
